import numpy as np
import ml_dtypes


def mxq(x, axis, fmt="e4m3"):
    dtype, down = {"e4m3": (ml_dtypes.float8_e4m3fn, 7), "e5m2": (ml_dtypes.float8_e5m2, 14)}[fmt]
    v = np.moveaxis(np.asarray(x, np.float32).astype(ml_dtypes.bfloat16).astype(np.float64), axis, -1)
    blocks = v.reshape(v.shape[:-1] + (-1, 32))
    amax = np.abs(blocks).max(-1, keepdims=True)
    byte = np.maximum(np.where(amax > 0, np.frexp(amax)[1] - 1 + 127, 0) - down, 1)
    scale = np.exp2(byte - 127.0)
    codes = (blocks / scale).astype(np.float32).astype(dtype).astype(np.float64)
    return np.moveaxis((codes * scale).reshape(v.shape), -1, axis)


WIDE = False


def mx_kscale(k):
    if not WIDE:
        return np.ones(k)
    levels = np.array([10, -10, 5, -5, 0])
    if k % 512:
        return np.exp2(np.random.permutation(np.resize(levels, k // 32))).repeat(32)
    a = np.empty((k // 512, 16))
    for p in range(k // 512):
        a[p, :8] = np.random.permutation(np.resize(levels, 8))
        for g in range(8):
            far = levels[np.abs(levels - a[p, g]) >= 10]
            a[p, g + 8] = far[np.random.randint(len(far))]
    return np.exp2(a.ravel()).repeat(32)


def f64(x):
    return np.asarray(x).astype(np.float64)


def striped(idx):
    return np.tile(idx.reshape(-1, 16).T, (8, 1)).astype(np.uint16)


def unstriped(offs):
    return offs[:16].T.reshape(-1).astype(np.int64)


def pack_weight(w):
    k, n = w.shape
    w = f64(np.asarray(w, np.float32).astype(ml_dtypes.bfloat16)).reshape(k // 32, 32, n)
    amax = np.abs(w).max(1)
    byte = np.clip(np.where(amax > 0, np.frexp(amax)[1] - 1 + 127 - 7, 1), 1, 254)
    scaled = (w * np.exp2(127.0 - byte)[:, None, :]).reshape(k, n).astype(np.float32)
    words = np.ascontiguousarray(scaled.reshape(k // 512, 128, 4, n).transpose(0, 1, 3, 2)).astype(ml_dtypes.float8_e4m3fn).view(np.uint8)
    return words, np.ascontiguousarray(byte.astype(np.uint8).reshape(k // 512, 16, n))


def unpack_weight(words, scales):
    g, p, n, _ = words.shape
    vals = np.ascontiguousarray(words).view(ml_dtypes.float8_e4m3fn).astype(np.float64) * np.repeat(np.exp2(scales.astype(np.float64) - 127.0), 8, axis=1)[..., None]
    return vals.transpose(0, 1, 3, 2).reshape(g * 512, n)


def planes(y):
    n, m = y.shape
    v = y.astype(np.float32).astype(ml_dtypes.bfloat16).astype(np.float64).reshape(n // 32, 32, m)
    top = np.abs(v).max(1)
    byte = np.clip(np.where(top > 0, np.frexp(top)[1] - 1 + 127 - 7, 1), 1, 254)
    codes = (v * np.exp2(127.0 - byte)[:, None, :]).reshape(n, m).astype(np.float32).astype(ml_dtypes.float8_e4m3fn).view(np.uint8)
    words = codes.reshape(n // 512, 128, 4, m).transpose(0, 1, 3, 2)
    return np.ascontiguousarray(words), np.ascontiguousarray(byte.astype(np.uint8).reshape(n // 512, 16, m))


def relu(v):
    return np.maximum(v, 0.0)


K, T, S, D, V, H, N = 1024, 2048, 1024, 2, 512, 512, 512
P = 2 ** 7


def setup_inputs():
    n = np.random.standard_normal
    s = mx_kscale(K)[:, None]
    u = mx_kscale(H)
    packed_xT = pack_weight(n((K, T)) * s)
    return {
        "x_words": packed_xT[0],
        "x_scales": packed_xT[1],
        "w1": (n((K, H)) / np.sqrt(K) / s * u).astype(np.float32),
        "w2": (n((H, N)) / np.sqrt(H) / u[:, None]).astype(np.float32),
        "gate": (np.tile(np.random.uniform(0.2, 1.0, (D, 1, V)), (1, P, 1))).astype(np.float32),
        "offs": striped(np.random.permutation(T)[:S]),
    }


def reference(x_words, x_scales, w1, w2, gate, offs):
    xq = unpack_weight(x_words, x_scales)[:, unstriped(offs)]
    w1q = mxq(f64(w1), 0, "e4m3")
    y0 = w1q.T @ xq[:, :V]
    y1 = w1q.T @ xq[:, V:2 * V]
    z = relu(y0 * f64(gate)[0, :1] + y1 * f64(gate)[1, :1])
    out_0 = mxq(f64(w2), 0, "e4m3").T @ mxq(z, 0, "e4m3")
    return (out_0,) + planes(out_0)

@@ -1,0 +1,187 @@
+from contextlib import ExitStack
+
+import concourse.mybir as mybir
+from concourse.masks import make_identity
+
+K, T, S, D, V, H, N = 1024, 2048, 1024, 2, 512, 512, 512
+FLOPS = 2 * K * H * S + 2 * H * N * V
+
+F32 = mybir.dt.float32
+BF16 = mybir.dt.bfloat16
+I32 = mybir.dt.int32
+U32 = mybir.dt.uint32
+U16 = mybir.dt.uint16
+U8 = mybir.dt.uint8
+FP8X4 = mybir.dt.float8_e4m3fn_x4
+ACT = mybir.ActivationFunctionType
+ALU = mybir.AluOpType
+
+P = 128
+PASSES = K // 512
+TILES = V // P
+SCALAR_SHARE = 44
+
+
+def tile_picked_zbloom_relu_po_kernel(
+    tc, x_words, x_scales, w1, w2, gate, offs, out_0, out_1, out_2
+):
+    nc = tc.nc
+    with ExitStack() as ctx:
+        keep = ctx.enter_context(tc.tile_pool(name="keep", bufs=1))
+        psum = ctx.enter_context(tc.psum_pool(name="psum", bufs=1))
+
+        def sb(name, shape, dtype):
+            return keep.tile(shape, dtype, name=name, align_bytes=64)
+
+        def bank(c, d, shape):
+            return psum.tile(shape, F32, name="bank", tag="bank%d%d" % (c, d))
+
+        offsets = keep.tile([P, S // 16], U16, name="offsets")
+        table_words = [sb("table_words%d" % o, [P, T], U32) for o in range(PASSES)]
+        table_scales = sb("table_scales", [P, T], U8)
+        w1_raw = [sb("w1_raw%d" % o, [P, 4, H], F32) for o in range(PASSES)]
+        w2_raw = sb("w2_raw", [P, 4, N], F32)
+        gate_rows = sb("gate_rows", [P, P], F32)
+        identity = sb("identity", [P, P], F32)
+
+        nc.gpsimd.memset(table_scales[:].bitcast(I32), 0)
+        nc.vector.memset(gate_rows[:], 0.0)
+        make_identity(nc, identity[:])
+
+        def load_words(o):
+            nc.sync.dma_start(
+                out=table_words[o][:].bitcast(I32),
+                in_=x_words[o].rearrange("p n t -> p (n t)").bitcast(I32),
+            )
+
+        def load_w1(o):
+            nc.sync.dma_start(
+                out=w1_raw[o][:], in_=w1[512 * o : 512 * (o + 1), :].rearrange("(p j) c -> p j c", j=4)
+            )
+
+        load_words(0)
+        nc.sync.dma_start(offsets[:], offs)
+        for q in range(4):
+            nc.sync.dma_start(
+                out=table_scales[32 * q : 32 * q + 8, :].bitcast(I32),
+                in_=x_scales[:, 4 * q : 4 * q + 4, :].bitcast(I32),
+            )
+        gate_flat = gate.rearrange("d r (c m) -> (d r c) m", m=P)
+        first = P * TILES - TILES
+        nc.scalar.dma_start(out=gate_rows[0 : D * TILES, :], in_=gate_flat[first : first + D * TILES, :])
+        load_w1(0)
+        load_words(1)
+        load_w1(1)
+        nc.sync.dma_start(out=w2_raw[:], in_=w2.rearrange("(p j) c -> p j c", j=4))
+
+        gate_turned = bank(TILES - 1, 1, [P, P])
+        nc.tensor.transpose(gate_turned[:], gate_rows[:], identity[:])
+        gates = sb("gates", [P, D * TILES], F32)
+        nc.scalar.activation(out=gates[:], in_=gate_turned[:, 0 : D * TILES], func=ACT.Copy)
+
+        picked_scales = sb("picked_scales", [P, S], U8)
+        nc.vector.tensor_copy(picked_scales[:], table_scales[:].indirect(offsets[:]))
+        picked_words = [[sb("picked_words%d%d" % (o, d), [P, V], U32) for d in range(D)] for o in range(PASSES)]
+
+        def gather_words(o):
+            for d in range(D):
+                nc.vector.tensor_copy(
+                    picked_words[o][d][:], table_words[o][:].indirect(offsets[:, d * V // 16 : (d + 1) * V // 16])
+                )
+
+        w1_codes = [sb("w1_codes%d" % o, [P, H], U32) for o in range(PASSES)]
+        w1_scales = [sb("w1_scales%d" % o, [P, H], U8) for o in range(PASSES)]
+
+        def quantise_w1(o):
+            rounded = sb("w1_rounded%d" % o, [P, 4 * H], BF16)
+            dst = rounded[:].rearrange("p (u m e j) -> p m j u e", u=2, e=2, j=4)
+            src = w1_raw[o][:].rearrange("p j (m u e) -> p m j u e", u=2, e=2)
+            nc.scalar.copy(out=dst[:, :SCALAR_SHARE], in_=src[:, :SCALAR_SHARE])
+            nc.vector.tensor_copy(out=dst[:, SCALAR_SHARE:], in_=src[:, SCALAR_SHARE:])
+            nc.vector.quantize_mx(out=w1_codes[o][:].bitcast(FP8X4), scales=w1_scales[o][:], in_=rounded[:])
+
+        y = [[bank(c, d, [P, H]) for d in range(D)] for c in range(TILES)]
+
+        def first_product(o, c, d):
+            cols = slice(P * c, P * (c + 1))
+            nc.tensor.matmul_mx(
+                out=y[c][d][:],
+                lhsT=picked_words[o][d][:, cols].bitcast(FP8X4),
+                lhsT_scale=picked_scales[4 * o :, V * d + P * c : V * d + P * (c + 1)],
+                rhs=w1_codes[o][:].bitcast(FP8X4),
+                rhs_scale=w1_scales[o][:],
+                start=(o == 0),
+                stop=(o == PASSES - 1),
+            )
+
+        for o in range(PASSES):
+            gather_words(o)
+            quantise_w1(o)
+            for c in range(TILES):
+                for d in range(D):
+                    first_product(o, c, d)
+
+        w2_codes = sb("w2_codes", [P, N], U32)
+        w2_scales = sb("w2_scales", [P, N], U8)
+        w2_rounded = sb("w2_rounded", [P, 4 * N], BF16)
+        nc.vector.tensor_copy(
+            out=w2_rounded[:].rearrange("p (t m j) -> p m j t", t=4, j=4),
+            in_=w2_raw[:].rearrange("p j (m t) -> p m j t", t=4),
+        )
+        nc.vector.quantize_mx(out=w2_codes[:].bitcast(FP8X4), scales=w2_scales[:], in_=w2_rounded[:])
+
+        out_codes = sb("out_codes", [P, V], U32)
+        out_scales = sb("out_scales", [P, V], U8)
+        out_rows = out_0.rearrange("(p t) v -> p t v", t=4)
+        out_words = out_1[0].rearrange("p c r -> p (c r)").bitcast(I32)
+
+        for c in range(TILES):
+            cols = slice(P * c, P * (c + 1))
+            term0 = sb("term0_%d" % c, [P, H], F32)
+            nc.scalar.activation(out=term0[:], in_=y[c][0][:], func=ACT.Copy, scale=gates[:, c : c + 1])
+            summed = sb("summed%d" % c, [P, H], BF16)
+            nc.vector.scalar_tensor_tensor(
+                out=summed[:], in0=y[c][1][:], scalar=gates[:, TILES + c : TILES + c + 1], in1=term0[:],
+                op0=ALU.mult, op1=ALU.add,
+            )
+            turned = bank(c, 0, [P, 2, P])
+            pairs = summed[:].bitcast(F32)
+            for u in range(2):
+                nc.tensor.transpose(turned[:, u, :], pairs[:, P * u : P * (u + 1)], identity[:])
+            z = sb("z%d" % c, [P, 4 * P], BF16)
+            nc.scalar.activation(
+                out=z[:].rearrange("p (v u e) -> p v u e", u=2, e=2),
+                in_=turned[:].bitcast(BF16).rearrange("p u (v e) -> p v u e", e=2),
+                func=ACT.Relu,
+            )
+            z_codes = sb("z_codes%d" % c, [P, P], U32)
+            z_scales = sb("z_scales%d" % c, [P, P], U8)
+            nc.vector.quantize_mx(out=z_codes[:].bitcast(FP8X4), scales=z_scales[:], in_=z[:])
+            result = bank(c, 1, [P, 4, P])
+            for t in range(4):
+                nc.tensor.matmul_mx(
+                    out=result[:, t, :],
+                    lhsT=w2_codes[:, P * t : P * (t + 1)].bitcast(FP8X4),
+                    lhsT_scale=w2_scales[:, P * t : P * (t + 1)],
+                    rhs=z_codes[:].bitcast(FP8X4),
+                    rhs_scale=z_scales[:],
+                    start=True,
+                    stop=True,
+                )
+            out_f32 = sb("out_f32_%d" % c, [P, 4, P], F32)
+            nc.scalar.copy(out=out_f32[:], in_=result[:])
+            nc.sync.dma_start(out=out_rows[:, :, cols], in_=out_f32[:])
+            out_rounded = sb("out_rounded%d" % c, [P, 4 * P], BF16)
+            nc.vector.tensor_copy(
+                out=out_rounded[:].rearrange("p (g i t) -> p g t i", i=4, t=4),
+                in_=out_f32[:].rearrange("p t (g i) -> p g t i", i=4),
+            )
+            nc.vector.quantize_mx(out=out_codes[:, cols].bitcast(FP8X4), scales=out_scales[:, cols], in_=out_rounded[:])
+            nc.sync.dma_start(out=out_words[:, cols], in_=out_codes[:, cols].bitcast(I32))
+
+        for q in range(4):
+            queue = nc.sync if q % 2 == 0 else nc.scalar
+            queue.dma_start(
+                out=out_2[0, 4 * q : 4 * q + 4, :].bitcast(I32),
+                in_=out_scales[32 * q : 32 * q + 4, :].bitcast(I32),
+            )

@@ -19,7 +19,6 @@ ALU = mybir.AluOpType
 P = 128
 PASSES = K // 512
 TILES = V // P
-SCALAR_SHARE = 44
 
 
 def tile_picked_zbloom_relu_po_kernel(
@@ -30,8 +29,8 @@ def tile_picked_zbloom_relu_po_kernel(
         keep = ctx.enter_context(tc.tile_pool(name="keep", bufs=1))
         psum = ctx.enter_context(tc.psum_pool(name="psum", bufs=1))
 
-        def sb(name, shape, dtype):
-            return keep.tile(shape, dtype, name=name, align_bytes=64)
+        def sb(name, shape, dtype, tag=""):
+            return keep.tile(shape, dtype, name=name, tag=tag or name, align_bytes=64)
 
         def bank(c, d, shape):
             return psum.tile(shape, F32, name="bank", tag="bank%d%d" % (c, d))
@@ -39,75 +38,100 @@ def tile_picked_zbloom_relu_po_kernel(
         offsets = keep.tile([P, S // 16], U16, name="offsets")
         table_words = [sb("table_words%d" % o, [P, T], U32) for o in range(PASSES)]
         table_scales = sb("table_scales", [P, T], U8)
-        w1_raw = [sb("w1_raw%d" % o, [P, 4, H], F32) for o in range(PASSES)]
-        w2_raw = sb("w2_raw", [P, 4, N], F32)
+        w1_raw = [[sb("w1_raw%d%d" % (o, h), [P, 4, H // 2], F32) for h in range(2)] for o in range(PASSES)]
+        w2_raw = [sb("w2_raw%d" % h, [P, 4, N // 2], F32) for h in range(2)]
         gate_rows = sb("gate_rows", [P, P], F32)
         identity = sb("identity", [P, P], F32)
 
-        nc.gpsimd.memset(table_scales[:].bitcast(I32), 0)
         nc.vector.memset(gate_rows[:], 0.0)
+        nc.gpsimd.memset(table_scales[:].bitcast(I32), 0)
         make_identity(nc, identity[:])
 
-        def load_words(o):
+        def load_words(o, cols):
             nc.sync.dma_start(
-                out=table_words[o][:].bitcast(I32),
-                in_=x_words[o].rearrange("p n t -> p (n t)").bitcast(I32),
+                out=table_words[o][:, cols].bitcast(I32),
+                in_=x_words[o].rearrange("p n t -> p (n t)").bitcast(I32)[:, cols],
             )
 
-        def load_w1(o):
-            nc.sync.dma_start(
-                out=w1_raw[o][:], in_=w1[512 * o : 512 * (o + 1), :].rearrange("(p j) c -> p j c", j=4)
-            )
+        def load_w1(o, h):
+            rows = w1.rearrange("(o p j) c -> o p j c", o=PASSES, j=4)[o]
+            nc.sync.dma_start(out=w1_raw[o][h][:], in_=rows[:, :, h * H // 2 : (h + 1) * H // 2])
 
-        load_words(0)
+        def load_scales(quadrants):
+            for o in range(PASSES):
+                for q in quadrants:
+                    nc.sync.dma_start(
+                        out=table_scales[32 * q + 4 * o : 32 * q + 4 * o + 4, :].bitcast(I32),
+                        in_=x_scales[o, 4 * q : 4 * q + 4, :].bitcast(I32),
+                    )
+
+        load_words(0, slice(0, T // 2))
+        load_scales((0, 2))
+        load_words(0, slice(T // 2, T))
         nc.sync.dma_start(offsets[:], offs)
-        for q in range(4):
-            nc.sync.dma_start(
-                out=table_scales[32 * q : 32 * q + 8, :].bitcast(I32),
-                in_=x_scales[:, 4 * q : 4 * q + 4, :].bitcast(I32),
-            )
+        load_w1(0, 0)
+        load_scales((1, 3))
+        load_w1(0, 1)
         gate_flat = gate.rearrange("d r (c m) -> (d r c) m", m=P)
         first = P * TILES - TILES
-        nc.scalar.dma_start(out=gate_rows[0 : D * TILES, :], in_=gate_flat[first : first + D * TILES, :])
-        load_w1(0)
-        load_words(1)
-        load_w1(1)
-        nc.sync.dma_start(out=w2_raw[:], in_=w2.rearrange("(p j) c -> p j c", j=4))
+        nc.sync.dma_start(out=gate_rows[0 : D * TILES, :], in_=gate_flat[first : first + D * TILES, :])
+        load_words(1, slice(0, T))
+        load_w1(1, 0)
+        load_w1(1, 1)
+        for h in range(2):
+            rows = w2.rearrange("(p j) c -> p j c", j=4)
+            nc.sync.dma_start(out=w2_raw[h][:], in_=rows[:, :, h * N // 2 : (h + 1) * N // 2])
 
+        w1_codes = [sb("w1_codes%d" % o, [P, H], U32) for o in range(PASSES)]
+        w1_scales = [sb("w1_scales%d" % o, [P, H], U8) for o in range(PASSES)]
+
+        def gather_words(o, picked):
+            for d in range(D):
+                nc.vector.tensor_copy(
+                    picked[:, V * d : V * (d + 1)],
+                    table_words[o][:].indirect(offsets[:, d * V // 16 : (d + 1) * V // 16]),
+                )
+
+        def dealt(rounded):
+            return rounded[:].rearrange("p (u m e j) -> p m j u e", u=2, e=2, j=4)
+
+        def undealt(raw):
+            return raw[:].rearrange("p j (m u e) -> p m j u e", u=2, e=2)
+
+        def round_w1(o, rounded):
+            for h in range(2):
+                nc.scalar.copy(out=dealt(rounded)[:, h * P // 2 : (h + 1) * P // 2], in_=undealt(w1_raw[o][h]))
+
+        def quantise_w1(o, rounded):
+            nc.vector.quantize_mx(out=w1_codes[o][:].bitcast(FP8X4), scales=w1_scales[o][:], in_=rounded[:])
+
+        picked0 = sb("picked0", [P, S], U32)
+        gather_words(0, picked0)
+        picked_scales = sb("picked_scales", [P, S], U8)
+        nc.vector.tensor_copy(picked_scales[:], table_scales[:].indirect(offsets[:]))
+        w1_rounded0 = sb("w1_rounded0", [P, 4 * H], BF16)
+        round_w1(0, w1_rounded0)
+        quantise_w1(0, w1_rounded0)
         gate_turned = bank(TILES - 1, 1, [P, P])
         nc.tensor.transpose(gate_turned[:], gate_rows[:], identity[:])
         gates = sb("gates", [P, D * TILES], F32)
         nc.scalar.activation(out=gates[:], in_=gate_turned[:, 0 : D * TILES], func=ACT.Copy)
 
-        picked_scales = sb("picked_scales", [P, S], U8)
-        nc.vector.tensor_copy(picked_scales[:], table_scales[:].indirect(offsets[:]))
-        picked_words = [[sb("picked_words%d%d" % (o, d), [P, V], U32) for d in range(D)] for o in range(PASSES)]
-
-        def gather_words(o):
-            for d in range(D):
-                nc.vector.tensor_copy(
-                    picked_words[o][d][:], table_words[o][:].indirect(offsets[:, d * V // 16 : (d + 1) * V // 16])
-                )
-
-        w1_codes = [sb("w1_codes%d" % o, [P, H], U32) for o in range(PASSES)]
-        w1_scales = [sb("w1_scales%d" % o, [P, H], U8) for o in range(PASSES)]
-
-        def quantise_w1(o):
-            rounded = sb("w1_rounded%d" % o, [P, 4 * H], BF16)
-            dst = rounded[:].rearrange("p (u m e j) -> p m j u e", u=2, e=2, j=4)
-            src = w1_raw[o][:].rearrange("p j (m u e) -> p m j u e", u=2, e=2)
-            nc.scalar.copy(out=dst[:, :SCALAR_SHARE], in_=src[:, :SCALAR_SHARE])
-            nc.vector.tensor_copy(out=dst[:, SCALAR_SHARE:], in_=src[:, SCALAR_SHARE:])
-            nc.vector.quantize_mx(out=w1_codes[o][:].bitcast(FP8X4), scales=w1_scales[o][:], in_=rounded[:])
+        picked1 = sb("picked1", [P, S], U32)
+        gather_words(1, picked1)
+        picked_words = [picked0, picked1]
+        w1_rounded1 = sb("w1_rounded1", [P, 4 * H], BF16, tag="rounded")
+        round_w1(1, w1_rounded1)
+        quantise_w1(1, w1_rounded1)
 
         y = [[bank(c, d, [P, H]) for d in range(D)] for c in range(TILES)]
 
         def first_product(o, c, d):
-            cols = slice(P * c, P * (c + 1))
+            entries = slice(V * d + P * c, V * d + P * (c + 1))
             nc.tensor.matmul_mx(
                 out=y[c][d][:],
-                lhsT=picked_words[o][d][:, cols].bitcast(FP8X4),
-                lhsT_scale=picked_scales[4 * o :, V * d + P * c : V * d + P * (c + 1)],
+                lhsT=picked_words[o][:, entries].bitcast(FP8X4),
+                lhsT_scale=picked_scales[4 * o :, entries],
                 rhs=w1_codes[o][:].bitcast(FP8X4),
                 rhs_scale=w1_scales[o][:],
                 start=(o == 0),
@@ -115,28 +139,20 @@ def tile_picked_zbloom_relu_po_kernel(
             )
 
         for o in range(PASSES):
-            gather_words(o)
-            quantise_w1(o)
             for c in range(TILES):
                 for d in range(D):
                     first_product(o, c, d)
 
-        w2_codes = sb("w2_codes", [P, N], U32)
         w2_scales = sb("w2_scales", [P, N], U8)
-        w2_rounded = sb("w2_rounded", [P, 4 * N], BF16)
-        nc.vector.tensor_copy(
-            out=w2_rounded[:].rearrange("p (t m j) -> p m j t", t=4, j=4),
-            in_=w2_raw[:].rearrange("p j (m t) -> p m j t", t=4),
-        )
-        nc.vector.quantize_mx(out=w2_codes[:].bitcast(FP8X4), scales=w2_scales[:], in_=w2_rounded[:])
+        w2_rounded = sb("w2_rounded", [P, 4 * N], BF16, tag="rounded")
+        for h in range(2):
+            nc.vector.tensor_copy(
+                out=w2_rounded[:].rearrange("p (t m j) -> p m j t", t=4, j=4)[:, h * P // 2 : (h + 1) * P // 2],
+                in_=w2_raw[h][:].rearrange("p j (m t) -> p m j t", t=4),
+            )
 
-        out_codes = sb("out_codes", [P, V], U32)
-        out_scales = sb("out_scales", [P, V], U8)
-        out_rows = out_0.rearrange("(p t) v -> p t v", t=4)
-        out_words = out_1[0].rearrange("p c r -> p (c r)").bitcast(I32)
-
+        turned = []
         for c in range(TILES):
-            cols = slice(P * c, P * (c + 1))
             term0 = sb("term0_%d" % c, [P, H], F32)
             nc.scalar.activation(out=term0[:], in_=y[c][0][:], func=ACT.Copy, scale=gates[:, c : c + 1])
             summed = sb("summed%d" % c, [P, H], BF16)
@@ -144,23 +160,30 @@ def tile_picked_zbloom_relu_po_kernel(
                 out=summed[:], in0=y[c][1][:], scalar=gates[:, TILES + c : TILES + c + 1], in1=term0[:],
                 op0=ALU.mult, op1=ALU.add,
             )
-            turned = bank(c, 0, [P, 2, P])
+            turned.append(bank(c, 0, [P, 2, P]))
             pairs = summed[:].bitcast(F32)
             for u in range(2):
-                nc.tensor.transpose(turned[:, u, :], pairs[:, P * u : P * (u + 1)], identity[:])
+                nc.tensor.transpose(turned[c][:, u, :], pairs[:, P * u : P * (u + 1)], identity[:])
+
+        w2_codes = sb("w2_codes", [P, N], U32, tag="term0_%d" % (TILES - 1))
+        nc.vector.quantize_mx(out=w2_codes[:].bitcast(FP8X4), scales=w2_scales[:], in_=w2_rounded[:])
+
+        result = []
+        for c in range(TILES):
             z = sb("z%d" % c, [P, 4 * P], BF16)
-            nc.scalar.activation(
-                out=z[:].rearrange("p (v u e) -> p v u e", u=2, e=2),
-                in_=turned[:].bitcast(BF16).rearrange("p u (v e) -> p v u e", e=2),
-                func=ACT.Relu,
-            )
+            z_view = z[:].rearrange("p (v u e) -> p v u e", u=2, e=2)
+            turned_view = turned[c][:].bitcast(BF16).rearrange("p u (v e) -> p v u e", e=2)
+            if c < TILES - 1:
+                nc.scalar.activation(out=z_view, in_=turned_view, func=ACT.Relu)
+            else:
+                nc.vector.tensor_scalar_max(out=z_view, in0=turned_view, scalar1=0.0)
             z_codes = sb("z_codes%d" % c, [P, P], U32)
             z_scales = sb("z_scales%d" % c, [P, P], U8)
             nc.vector.quantize_mx(out=z_codes[:].bitcast(FP8X4), scales=z_scales[:], in_=z[:])
-            result = bank(c, 1, [P, 4, P])
+            result.append(bank(c, 1, [P, 4, P]))
             for t in range(4):
                 nc.tensor.matmul_mx(
-                    out=result[:, t, :],
+                    out=result[c][:, t, :],
                     lhsT=w2_codes[:, P * t : P * (t + 1)].bitcast(FP8X4),
                     lhsT_scale=w2_scales[:, P * t : P * (t + 1)],
                     rhs=z_codes[:].bitcast(FP8X4),
@@ -168,19 +191,53 @@ def tile_picked_zbloom_relu_po_kernel(
                     start=True,
                     stop=True,
                 )
-            out_f32 = sb("out_f32_%d" % c, [P, 4, P], F32)
-            nc.scalar.copy(out=out_f32[:], in_=result[:])
-            nc.sync.dma_start(out=out_rows[:, :, cols], in_=out_f32[:])
-            out_rounded = sb("out_rounded%d" % c, [P, 4 * P], BF16)
-            nc.vector.tensor_copy(
-                out=out_rounded[:].rearrange("p (g i t) -> p g t i", i=4, t=4),
-                in_=out_f32[:].rearrange("p t (g i) -> p g t i", i=4),
-            )
-            nc.vector.quantize_mx(out=out_codes[:, cols].bitcast(FP8X4), scales=out_scales[:, cols], in_=out_rounded[:])
-            nc.sync.dma_start(out=out_words[:, cols], in_=out_codes[:, cols].bitcast(I32))
 
+        out_codes = sb("out_codes", [P, V], U32)
+        out_scales = sb("out_scales", [P, V], U8)
+        out_rows = out_0.rearrange("(p t) v -> p t v", t=4)
+        out_words = out_1[0].rearrange("p c r -> p (c r)").bitcast(I32)
+        out_f32 = [sb("out_f32_%d" % c, [P, 4, P], F32) for c in range(TILES)]
+        out_rounded = [sb("out_rounded%d" % c, [P, 4 * P], BF16) for c in range(TILES)]
+
+        def store_result(c):
+            nc.scalar.copy(out=out_f32[c][:], in_=result[c][:])
+            nc.sync.dma_start(out=out_rows[:, :, P * c : P * (c + 1)], in_=out_f32[c][:])
+
+        def round_result(c, source):
+            nc.vector.tensor_copy(
+                out=out_rounded[c][:].rearrange("p (g i t) -> p g t i", i=4, t=4),
+                in_=source[:].rearrange("p t (g i) -> p g t i", i=4),
+            )
+
+        def round_from_bank(c):
+            nc.vector.tensor_copy(
+                out=out_rounded[c][:].rearrange("p (v t) -> p v t", t=4),
+                in_=result[c][:].rearrange("p t v -> p v t"),
+            )
+
+        def quantise_result(c):
+            cols = slice(P * c, P * (c + 1))
+            nc.vector.quantize_mx(
+                out=out_codes[:, cols].bitcast(FP8X4), scales=out_scales[:, cols], in_=out_rounded[c][:]
+            )
+
+        last = TILES - 1
+        store_result(0)
+        round_result(0, out_f32[0])
+        round_from_bank(last)
+        quantise_result(0)
+        store_result(1)
+        round_result(1, out_f32[1])
+        quantise_result(last)
+        store_result(2)
+        round_result(2, out_f32[2])
+        store_result(last)
+        quantise_result(1)
+        quantise_result(2)
+
+        nc.sync.dma_start(out=out_words, in_=out_codes[:].bitcast(I32))
         for q in range(4):
-            queue = nc.sync if q % 2 == 0 else nc.scalar
+            queue = nc.sync if q == 0 else nc.scalar
             queue.dma_start(
                 out=out_2[0, 4 * q : 4 * q + 4, :].bitcast(I32),
                 in_=out_scales[32 * q : 32 * q + 4, :].bitcast(I32),

@@ -19,6 +19,7 @@ ALU = mybir.AluOpType
 P = 128
 PASSES = K // 512
 TILES = V // P
+EARLY = 768
 
 
 def tile_picked_zbloom_relu_po_kernel(
@@ -107,11 +108,13 @@ def tile_picked_zbloom_relu_po_kernel(
 
         picked0 = sb("picked0", [P, S], U32)
         gather_words(0, picked0)
-        picked_scales = sb("picked_scales", [P, S], U8)
-        nc.vector.tensor_copy(picked_scales[:], table_scales[:].indirect(offsets[:]))
-        w1_rounded0 = sb("w1_rounded0", [P, 4 * H], BF16)
+        early_scales = sb("early_scales", [P, EARLY], U8)
+        nc.vector.tensor_copy(early_scales[:], table_scales[:].indirect(offsets[:, : EARLY // 16]))
+        w1_rounded0 = sb("w1_rounded0", [P, 4 * H], BF16, tag="shared")
         round_w1(0, w1_rounded0)
         quantise_w1(0, w1_rounded0)
+        late_scales = sb("late_scales", [P, S - EARLY], U8, tag="shared")
+        nc.vector.tensor_copy(late_scales[:], table_scales[:].indirect(offsets[:, EARLY // 16 :]))
         gate_turned = bank(TILES - 1, 1, [P, P])
         nc.tensor.transpose(gate_turned[:], gate_rows[:], identity[:])
         gates = sb("gates", [P, D * TILES], F32)
@@ -120,36 +123,45 @@ def tile_picked_zbloom_relu_po_kernel(
         picked1 = sb("picked1", [P, S], U32)
         gather_words(1, picked1)
         picked_words = [picked0, picked1]
-        w1_rounded1 = sb("w1_rounded1", [P, 4 * H], BF16, tag="rounded")
+        w1_rounded1 = sb("w1_rounded1", [P, 4 * H], BF16)
         round_w1(1, w1_rounded1)
         quantise_w1(1, w1_rounded1)
 
         y = [[bank(c, d, [P, H]) for d in range(D)] for c in range(TILES)]
 
         def first_product(o, c, d):
-            entries = slice(V * d + P * c, V * d + P * (c + 1))
+            entry = V * d + P * c
+            entries = slice(entry, entry + P)
+            if entry < EARLY:
+                plane = early_scales[4 * o :, entries]
+            else:
+                plane = late_scales[4 * o :, entry - EARLY : entry - EARLY + P]
             nc.tensor.matmul_mx(
                 out=y[c][d][:],
                 lhsT=picked_words[o][:, entries].bitcast(FP8X4),
-                lhsT_scale=picked_scales[4 * o :, entries],
+                lhsT_scale=plane,
                 rhs=w1_codes[o][:].bitcast(FP8X4),
                 rhs_scale=w1_scales[o][:],
                 start=(o == 0),
                 stop=(o == PASSES - 1),
             )
 
-        for o in range(PASSES):
+        for d in range(D):
             for c in range(TILES):
-                for d in range(D):
-                    first_product(o, c, d)
+                first_product(0, c, d)
+        for c in range(TILES):
+            for d in range(D):
+                first_product(1, c, d)
 
         w2_scales = sb("w2_scales", [P, N], U8)
-        w2_rounded = sb("w2_rounded", [P, 4 * N], BF16, tag="rounded")
-        for h in range(2):
-            nc.vector.tensor_copy(
-                out=w2_rounded[:].rearrange("p (t m j) -> p m j t", t=4, j=4)[:, h * P // 2 : (h + 1) * P // 2],
-                in_=w2_raw[h][:].rearrange("p j (m t) -> p m j t", t=4),
-            )
+        w2_rounded = sb("w2_rounded", [P, 4 * N], BF16)
+        w2_dealt = w2_rounded[:].rearrange("p (t m j) -> p m j t", t=4, j=4)
+        w2_halves = [raw[:].rearrange("p j (m t) -> p m j t", t=4) for raw in w2_raw]
+        half = P // 2
+        nc.scalar.copy(out=w2_dealt[:, :half], in_=w2_halves[0])
+        nc.vector.tensor_copy(out=w2_dealt[:, half:], in_=w2_halves[1])
+        w2_codes = sb("w2_codes", [P, N], U32)
+        nc.vector.quantize_mx(out=w2_codes[:].bitcast(FP8X4), scales=w2_scales[:], in_=w2_rounded[:])
 
         turned = []
         for c in range(TILES):
@@ -164,9 +176,6 @@ def tile_picked_zbloom_relu_po_kernel(
             pairs = summed[:].bitcast(F32)
             for u in range(2):
                 nc.tensor.transpose(turned[c][:, u, :], pairs[:, P * u : P * (u + 1)], identity[:])
-
-        w2_codes = sb("w2_codes", [P, N], U32, tag="term0_%d" % (TILES - 1))
-        nc.vector.quantize_mx(out=w2_codes[:].bitcast(FP8X4), scales=w2_scales[:], in_=w2_rounded[:])
 
         result = []
         for c in range(TILES):

from contextlib import ExitStack

import concourse.mybir as mybir
from concourse.masks import make_identity

K, T, S, D, V, H, N = 1024, 2048, 1024, 2, 512, 512, 512
FLOPS = 2 * K * H * S + 2 * H * N * V

F32 = mybir.dt.float32
BF16 = mybir.dt.bfloat16
I32 = mybir.dt.int32
U32 = mybir.dt.uint32
U16 = mybir.dt.uint16
U8 = mybir.dt.uint8
FP8X4 = mybir.dt.float8_e4m3fn_x4
ACT = mybir.ActivationFunctionType
ALU = mybir.AluOpType

P = 128
PASSES = K // 512
TILES = V // P
EARLY = 768


def tile_picked_zbloom_relu_po_kernel(
    tc, x_words, x_scales, w1, w2, gate, offs, out_0, out_1, out_2
):
    nc = tc.nc
    with ExitStack() as ctx:
        keep = ctx.enter_context(tc.tile_pool(name="keep", bufs=1))
        psum = ctx.enter_context(tc.psum_pool(name="psum", bufs=1))

        def sb(name, shape, dtype, tag=""):
            return keep.tile(shape, dtype, name=name, tag=tag or name, align_bytes=64)

        def bank(c, d, shape):
            return psum.tile(shape, F32, name="bank", tag="bank%d%d" % (c, d))

        offsets = keep.tile([P, S // 16], U16, name="offsets")
        table_words = [sb("table_words%d" % o, [P, T], U32) for o in range(PASSES)]
        table_scales = sb("table_scales", [P, T], U8)
        w1_raw = [[sb("w1_raw%d%d" % (o, h), [P, 4, H // 2], F32) for h in range(2)] for o in range(PASSES)]
        w2_raw = [sb("w2_raw%d" % h, [P, 4, N // 2], F32) for h in range(2)]
        gate_rows = sb("gate_rows", [P, P], F32)
        identity = sb("identity", [P, P], F32)

        nc.vector.memset(gate_rows[:], 0.0)
        nc.gpsimd.memset(table_scales[:].bitcast(I32), 0)
        make_identity(nc, identity[:])

        def load_words(o, cols):
            nc.sync.dma_start(
                out=table_words[o][:, cols].bitcast(I32),
                in_=x_words[o].rearrange("p n t -> p (n t)").bitcast(I32)[:, cols],
            )

        def load_w1(o, h):
            rows = w1.rearrange("(o p j) c -> o p j c", o=PASSES, j=4)[o]
            nc.sync.dma_start(out=w1_raw[o][h][:], in_=rows[:, :, h * H // 2 : (h + 1) * H // 2])

        def load_scales(quadrants):
            for o in range(PASSES):
                for q in quadrants:
                    nc.sync.dma_start(
                        out=table_scales[32 * q + 4 * o : 32 * q + 4 * o + 4, :].bitcast(I32),
                        in_=x_scales[o, 4 * q : 4 * q + 4, :].bitcast(I32),
                    )

        load_words(0, slice(0, T // 2))
        load_scales((0, 2))
        load_words(0, slice(T // 2, T))
        nc.sync.dma_start(offsets[:], offs)
        load_w1(0, 0)
        load_scales((1, 3))
        load_w1(0, 1)
        gate_flat = gate.rearrange("d r (c m) -> (d r c) m", m=P)
        first = P * TILES - TILES
        nc.sync.dma_start(out=gate_rows[0 : D * TILES, :], in_=gate_flat[first : first + D * TILES, :])
        load_words(1, slice(0, T))
        load_w1(1, 0)
        load_w1(1, 1)
        for h in range(2):
            rows = w2.rearrange("(p j) c -> p j c", j=4)
            nc.sync.dma_start(out=w2_raw[h][:], in_=rows[:, :, h * N // 2 : (h + 1) * N // 2])

        w1_codes = [sb("w1_codes%d" % o, [P, H], U32) for o in range(PASSES)]
        w1_scales = [sb("w1_scales%d" % o, [P, H], U8) for o in range(PASSES)]

        def gather_words(o, picked):
            for d in range(D):
                nc.vector.tensor_copy(
                    picked[:, V * d : V * (d + 1)],
                    table_words[o][:].indirect(offsets[:, d * V // 16 : (d + 1) * V // 16]),
                )

        def dealt(rounded):
            return rounded[:].rearrange("p (u m e j) -> p m j u e", u=2, e=2, j=4)

        def undealt(raw):
            return raw[:].rearrange("p j (m u e) -> p m j u e", u=2, e=2)

        def round_w1(o, rounded):
            for h in range(2):
                nc.scalar.copy(out=dealt(rounded)[:, h * P // 2 : (h + 1) * P // 2], in_=undealt(w1_raw[o][h]))

        def quantise_w1(o, rounded):
            nc.vector.quantize_mx(out=w1_codes[o][:].bitcast(FP8X4), scales=w1_scales[o][:], in_=rounded[:])

        picked0 = sb("picked0", [P, S], U32)
        gather_words(0, picked0)
        early_scales = sb("early_scales", [P, EARLY], U8)
        nc.vector.tensor_copy(early_scales[:], table_scales[:].indirect(offsets[:, : EARLY // 16]))
        w1_rounded0 = sb("w1_rounded0", [P, 4 * H], BF16, tag="shared")
        round_w1(0, w1_rounded0)
        quantise_w1(0, w1_rounded0)
        late_scales = sb("late_scales", [P, S - EARLY], U8, tag="shared")
        nc.vector.tensor_copy(late_scales[:], table_scales[:].indirect(offsets[:, EARLY // 16 :]))
        gate_turned = bank(TILES - 1, 1, [P, P])
        nc.tensor.transpose(gate_turned[:], gate_rows[:], identity[:])
        gates = sb("gates", [P, D * TILES], F32)
        nc.scalar.activation(out=gates[:], in_=gate_turned[:, 0 : D * TILES], func=ACT.Copy)

        picked1 = sb("picked1", [P, S], U32)
        gather_words(1, picked1)
        picked_words = [picked0, picked1]
        w1_rounded1 = sb("w1_rounded1", [P, 4 * H], BF16)
        round_w1(1, w1_rounded1)
        quantise_w1(1, w1_rounded1)

        y = [[bank(c, d, [P, H]) for d in range(D)] for c in range(TILES)]

        def first_product(o, c, d):
            entry = V * d + P * c
            entries = slice(entry, entry + P)
            if entry < EARLY:
                plane = early_scales[4 * o :, entries]
            else:
                plane = late_scales[4 * o :, entry - EARLY : entry - EARLY + P]
            nc.tensor.matmul_mx(
                out=y[c][d][:],
                lhsT=picked_words[o][:, entries].bitcast(FP8X4),
                lhsT_scale=plane,
                rhs=w1_codes[o][:].bitcast(FP8X4),
                rhs_scale=w1_scales[o][:],
                start=(o == 0),
                stop=(o == PASSES - 1),
            )

        for d in range(D):
            for c in range(TILES):
                first_product(0, c, d)
        for c in range(TILES):
            for d in range(D):
                first_product(1, c, d)

        w2_scales = sb("w2_scales", [P, N], U8)
        w2_rounded = sb("w2_rounded", [P, 4 * N], BF16)
        w2_dealt = w2_rounded[:].rearrange("p (t m j) -> p m j t", t=4, j=4)
        w2_halves = [raw[:].rearrange("p j (m t) -> p m j t", t=4) for raw in w2_raw]
        half = P // 2
        nc.scalar.copy(out=w2_dealt[:, :half], in_=w2_halves[0])
        nc.vector.tensor_copy(out=w2_dealt[:, half:], in_=w2_halves[1])
        w2_codes = sb("w2_codes", [P, N], U32)
        nc.vector.quantize_mx(out=w2_codes[:].bitcast(FP8X4), scales=w2_scales[:], in_=w2_rounded[:])

        turned = []
        for c in range(TILES):
            term0 = sb("term0_%d" % c, [P, H], F32)
            nc.scalar.activation(out=term0[:], in_=y[c][0][:], func=ACT.Copy, scale=gates[:, c : c + 1])
            summed = sb("summed%d" % c, [P, H], BF16)
            nc.vector.scalar_tensor_tensor(
                out=summed[:], in0=y[c][1][:], scalar=gates[:, TILES + c : TILES + c + 1], in1=term0[:],
                op0=ALU.mult, op1=ALU.add,
            )
            turned.append(bank(c, 0, [P, 2, P]))
            pairs = summed[:].bitcast(F32)
            for u in range(2):
                nc.tensor.transpose(turned[c][:, u, :], pairs[:, P * u : P * (u + 1)], identity[:])

        result = []
        for c in range(TILES):
            z = sb("z%d" % c, [P, 4 * P], BF16)
            z_view = z[:].rearrange("p (v u e) -> p v u e", u=2, e=2)
            turned_view = turned[c][:].bitcast(BF16).rearrange("p u (v e) -> p v u e", e=2)
            if c < TILES - 1:
                nc.scalar.activation(out=z_view, in_=turned_view, func=ACT.Relu)
            else:
                nc.vector.tensor_scalar_max(out=z_view, in0=turned_view, scalar1=0.0)
            z_codes = sb("z_codes%d" % c, [P, P], U32)
            z_scales = sb("z_scales%d" % c, [P, P], U8)
            nc.vector.quantize_mx(out=z_codes[:].bitcast(FP8X4), scales=z_scales[:], in_=z[:])
            result.append(bank(c, 1, [P, 4, P]))
            for t in range(4):
                nc.tensor.matmul_mx(
                    out=result[c][:, t, :],
                    lhsT=w2_codes[:, P * t : P * (t + 1)].bitcast(FP8X4),
                    lhsT_scale=w2_scales[:, P * t : P * (t + 1)],
                    rhs=z_codes[:].bitcast(FP8X4),
                    rhs_scale=z_scales[:],
                    start=True,
                    stop=True,
                )

        out_codes = sb("out_codes", [P, V], U32)
        out_scales = sb("out_scales", [P, V], U8)
        out_rows = out_0.rearrange("(p t) v -> p t v", t=4)
        out_words = out_1[0].rearrange("p c r -> p (c r)").bitcast(I32)
        out_f32 = [sb("out_f32_%d" % c, [P, 4, P], F32) for c in range(TILES)]
        out_rounded = [sb("out_rounded%d" % c, [P, 4 * P], BF16) for c in range(TILES)]

        def store_result(c):
            nc.scalar.copy(out=out_f32[c][:], in_=result[c][:])
            nc.sync.dma_start(out=out_rows[:, :, P * c : P * (c + 1)], in_=out_f32[c][:])

        def round_result(c, source):
            nc.vector.tensor_copy(
                out=out_rounded[c][:].rearrange("p (g i t) -> p g t i", i=4, t=4),
                in_=source[:].rearrange("p t (g i) -> p g t i", i=4),
            )

        def round_from_bank(c):
            nc.vector.tensor_copy(
                out=out_rounded[c][:].rearrange("p (v t) -> p v t", t=4),
                in_=result[c][:].rearrange("p t v -> p v t"),
            )

        def quantise_result(c):
            cols = slice(P * c, P * (c + 1))
            nc.vector.quantize_mx(
                out=out_codes[:, cols].bitcast(FP8X4), scales=out_scales[:, cols], in_=out_rounded[c][:]
            )

        last = TILES - 1
        store_result(0)
        round_result(0, out_f32[0])
        round_from_bank(last)
        quantise_result(0)
        store_result(1)
        round_result(1, out_f32[1])
        quantise_result(last)
        store_result(2)
        round_result(2, out_f32[2])
        store_result(last)
        quantise_result(1)
        quantise_result(2)

        nc.sync.dma_start(out=out_words, in_=out_codes[:].bitcast(I32))
        for q in range(4):
            queue = nc.sync if q == 0 else nc.scalar
            queue.dma_start(
                out=out_2[0, 4 * q : 4 * q + 4, :].bitcast(I32),
                in_=out_scales[32 * q : 32 * q + 4, :].bitcast(I32),
            )
